import numpy as np
CORES = [388,396,404,412,420,428,436,444,452,460,468,476,484,492,500,508,124,252,380]
N = 19
T = 256
ROUTE = [[[13],[15],[6],[13],[16],[11],[15],[17],[1],[6],[8],[13],[9],[2],[10],[1],[17],[5],[9],[3],[1],[11],[17],[7],[15],[18],[15],[2],[14],[15],[7],[2],[12],[8],[8],[15],[6],[12],[16],[8],[12],[17],[8],[16],[17],[8],[1],[10],[2],[16],[9],[7],[4],[7],[1],[8],[15],[2],[0],[18],[7],[3],[8],[11],[16],[6],[0],[1],[6],[4],[4],[15],[1],[18],[18],[1],[3],[2],[12],[15],[9],[14],[7],[18],[5],[2],[7],[14],[13],[8],[13],[9],[0],[5],[16],[12],[7],[5],[14],[7],[11],[11],[11],[10],[6],[6],[17],[6],[17],[3],[17],[14],[4],[1],[4],[5],[14],[4],[2],[2],[4],[8],[12],[9],[0],[6],[5],[2],[2],[18],[15],[5],[3],[8],[10],[17],[8],[9],[15],[2],[9],[8],[16],[14],[18],[17],[14],[14],[6],[13],[0],[2],[7],[0],[3],[8],[6],[10],[11],[16],[14],[10],[3],[10],[10],[9],[8],[9],[3],[2],[13],[14],[8],[7],[12],[6],[14],[3],[9],[16],[1],[5],[10],[0],[1],[4],[10],[18],[13],[0],[13],[15],[4],[4],[6],[9],[1],[8],[17],[3],[10],[13],[9],[8],[3],[6],[10],[17],[13],[13],[12],[6],[17],[15],[14],[14],[15],[11],[1],[16],[12],[2],[15],[9],[17],[14],[13],[17],[13],[1],[13],[17],[9],[5],[17],[1],[3],[6],[1],[12],[17],[11],[0],[4],[13],[18],[15],[10],[4],[9],[6],[12],[15],[5],[14],[10]],[[4],[7],[18],[1],[12],[12],[10],[0],[11],[12],[7],[11],[12],[11],[2],[15],[12],[4],[11],[8],[13],[8],[3],[11],[12],[2],[2],[15],[5],[16],[14],[16],[2],[16],[10],[8],[16],[3],[15],[12],[17],[7],[4],[6],[2],[11],[5],[5],[13],[7],[17],[13],[17],[8],[0],[10],[0],[4],[14],[9],[1],[7],[13],[4],[2],[3],[4],[5],[2],[14],[11],[17],[16],[18],[6],[15],[15],[7],[8],[11],[14],[11],[12],[12],[16],[6],[9],[3],[10],[11],[6],[6],[7],[13],[15],[5],[9],[17],[18],[5],[8],[4],[18],[18],[16],[1],[12],[1],[16],[5],[13],[0],[8],[11],[2],[5],[8],[3],[11],[10],[12],[18],[1],[11],[8],[6],[1],[16],[13],[18],[18],[9],[15],[15],[1],[6],[10],[5],[18],[4],[16],[14],[0],[12],[4],[7],[15],[2],[18],[16],[13],[16],[12],[2],[10],[1],[0],[9],[8],[13],[4],[3],[8],[0],[2],[5],[18],[18],[9],[2],[9],[15],[7],[7],[5],[15],[13],[0],[10],[7],[16],[8],[4],[2],[3],[16],[18],[3],[8],[13],[11],[15],[2],[1],[17],[15],[12],[15],[3],[0],[8],[18],[2],[7],[18],[18],[3],[12],[1],[5],[9],[14],[17],[18],[9],[2],[6],[11],[0],[18],[17],[5],[2],[10],[11],[4],[2],[2],[17],[5],[5],[2],[11],[10],[4],[8],[5],[1],[12],[2],[12],[2],[14],[9],[18],[3],[4],[5],[18],[1],[17],[11],[2],[0],[3],[5]],[[5],[8],[13],[15],[6],[13],[17],[18],[11],[11],[15],[9],[18],[1],[18],[10],[10],[1],[1],[5],[12],[2],[0],[17],[15],[10],[16],[2],[18],[0],[8],[13],[7],[3],[2],[1],[3],[8],[5],[3],[2],[15],[12],[2],[13],[12],[18],[4],[15],[4],[18],[18],[3],[12],[1],[1],[10],[6],[5],[15],[11],[15],[10],[7],[4],[14],[4],[7],[16],[1],[17],[15],[4],[9],[13],[1],[17],[16],[18],[12],[9],[2],[5],[17],[1],[11],[4],[5],[5],[5],[8],[4],[13],[17],[18],[9],[2],[7],[7],[11],[16],[2],[8],[5],[15],[8],[6],[13],[5],[6],[5],[14],[13],[15],[10],[5],[14],[9],[15],[4],[13],[6],[7],[13],[8],[8],[8],[0],[0],[4],[16],[5],[11],[15],[12],[6],[16],[12],[15],[6],[16],[14],[4],[17],[2],[9],[1],[1],[8],[1],[16],[2],[0],[2],[11],[8],[8],[14],[5],[7],[8],[1],[4],[1],[0],[18],[14],[2],[18],[1],[14],[16],[14],[12],[15],[17],[11],[6],[14],[7],[6],[3],[13],[17],[9],[16],[1],[10],[11],[12],[16],[10],[13],[5],[0],[4],[9],[1],[18],[15],[6],[5],[17],[15],[4],[1],[2],[8],[2],[7],[10],[4],[7],[3],[3],[11],[7],[2],[17],[9],[10],[18],[11],[11],[12],[12],[13],[8],[6],[15],[7],[15],[9],[3],[11],[16],[6],[18],[18],[13],[5],[13],[6],[0],[17],[5],[2],[8],[15],[0],[6],[4],[2],[2],[6],[2]],[[17],[18],[10],[14],[0],[14],[6],[12],[13],[17],[2],[8],[5],[12],[1],[14],[6],[5],[13],[4],[7],[1],[14],[14],[9],[16],[14],[7],[12],[12],[10],[15],[9],[9],[15],[4],[2],[12],[14],[10],[3],[7],[10],[12],[18],[17],[15],[14],[7],[17],[7],[1],[17],[14],[12],[0],[16],[17],[14],[14],[8],[13],[6],[18],[14],[0],[1],[14],[16],[5],[0],[13],[3],[7],[10],[0],[11],[13],[11],[3],[0],[6],[2],[5],[15],[4],[17],[4],[9],[7],[14],[14],[14],[10],[3],[4],[8],[18],[13],[0],[0],[1],[1],[10],[8],[12],[4],[13],[17],[12],[12],[18],[1],[0],[9],[0],[3],[4],[18],[17],[6],[4],[1],[12],[3],[15],[4],[4],[9],[11],[0],[12],[0],[9],[15],[12],[16],[5],[15],[5],[7],[0],[9],[17],[7],[6],[2],[14],[13],[12],[0],[5],[16],[11],[17],[12],[13],[0],[6],[13],[13],[2],[4],[1],[6],[1],[1],[4],[9],[15],[8],[7],[9],[7],[11],[12],[13],[3],[13],[0],[14],[5],[17],[15],[18],[16],[18],[4],[18],[6],[17],[10],[14],[17],[5],[13],[16],[6],[6],[18],[18],[10],[1],[16],[10],[1],[7],[3],[11],[3],[14],[11],[0],[3],[13],[1],[17],[15],[14],[5],[15],[12],[3],[13],[16],[16],[5],[10],[9],[9],[5],[6],[16],[2],[8],[13],[12],[1],[11],[14],[18],[16],[13],[7],[11],[17],[13],[16],[10],[0],[9],[7],[4],[15],[7],[8]],[[13],[7],[16],[5],[10],[13],[7],[14],[4],[8],[4],[9],[7],[11],[0],[9],[12],[14],[10],[17],[7],[4],[4],[7],[7],[13],[14],[3],[11],[6],[2],[8],[9],[11],[15],[14],[17],[9],[8],[4],[14],[6],[18],[2],[8],[17],[16],[13],[18],[15],[16],[14],[6],[12],[15],[14],[9],[4],[12],[18],[9],[13],[2],[4],[11],[12],[8],[0],[3],[17],[13],[18],[8],[3],[2],[0],[2],[13],[9],[7],[2],[8],[14],[4],[2],[14],[16],[18],[10],[18],[10],[1],[7],[7],[8],[3],[16],[0],[18],[9],[5],[13],[7],[10],[18],[5],[0],[7],[14],[12],[7],[13],[12],[4],[18],[16],[17],[14],[1],[10],[5],[8],[6],[2],[16],[14],[14],[8],[18],[14],[5],[3],[16],[1],[15],[14],[14],[8],[10],[18],[13],[17],[14],[8],[11],[1],[5],[4],[2],[4],[7],[15],[11],[18],[14],[3],[5],[12],[11],[6],[16],[5],[16],[11],[6],[18],[0],[8],[8],[15],[3],[6],[17],[16],[6],[14],[14],[0],[18],[5],[4],[11],[7],[18],[17],[14],[15],[8],[3],[4],[5],[11],[8],[4],[14],[10],[16],[9],[18],[1],[15],[3],[13],[4],[6],[5],[18],[12],[5],[3],[2],[7],[9],[6],[16],[0],[9],[14],[1],[0],[17],[2],[1],[3],[0],[4],[6],[13],[18],[9],[11],[4],[12],[10],[6],[7],[12],[3],[1],[8],[9],[18],[13],[11],[3],[14],[18],[14],[12],[3],[9],[18],[11],[16],[8],[16]],[[18],[1],[1],[0],[13],[18],[15],[7],[6],[11],[15],[1],[10],[4],[2],[1],[13],[8],[11],[12],[13],[8],[14],[17],[6],[6],[17],[12],[4],[8],[2],[11],[7],[1],[17],[17],[7],[0],[17],[17],[12],[6],[10],[7],[12],[14],[6],[17],[7],[15],[2],[7],[4],[7],[3],[16],[5],[8],[3],[13],[1],[5],[10],[18],[17],[6],[2],[3],[4],[13],[8],[4],[7],[5],[2],[1],[3],[12],[18],[0],[11],[6],[13],[2],[3],[6],[15],[18],[11],[9],[12],[1],[0],[16],[13],[2],[0],[17],[18],[11],[14],[9],[15],[14],[3],[14],[7],[10],[11],[2],[17],[15],[4],[16],[10],[2],[17],[2],[2],[1],[15],[14],[15],[13],[11],[2],[13],[13],[9],[9],[10],[16],[13],[11],[18],[4],[8],[6],[17],[7],[18],[18],[3],[8],[8],[12],[5],[7],[12],[4],[5],[0],[8],[6],[14],[9],[5],[16],[2],[18],[17],[0],[15],[9],[4],[3],[8],[15],[18],[4],[0],[8],[16],[15],[1],[17],[2],[14],[13],[17],[10],[8],[17],[5],[0],[16],[15],[0],[4],[13],[9],[4],[8],[16],[3],[18],[4],[4],[13],[18],[6],[16],[15],[2],[6],[11],[3],[1],[14],[14],[1],[17],[11],[14],[16],[7],[6],[2],[3],[17],[12],[2],[14],[2],[16],[6],[14],[7],[14],[0],[11],[12],[2],[17],[15],[10],[12],[12],[4],[3],[13],[0],[14],[6],[11],[12],[8],[7],[9],[7],[14],[5],[13],[6],[11],[13]],[[16],[6],[8],[17],[16],[0],[2],[8],[0],[1],[11],[9],[5],[14],[12],[4],[6],[3],[18],[2],[10],[5],[2],[18],[6],[13],[16],[5],[5],[7],[4],[9],[10],[5],[1],[6],[11],[16],[2],[12],[12],[4],[14],[6],[11],[18],[13],[9],[12],[5],[4],[10],[10],[14],[1],[13],[13],[13],[14],[14],[1],[8],[17],[9],[13],[2],[18],[15],[7],[13],[9],[5],[9],[16],[9],[15],[5],[0],[8],[6],[18],[18],[9],[0],[10],[12],[0],[6],[2],[15],[1],[7],[8],[14],[12],[8],[8],[2],[5],[12],[13],[11],[13],[14],[12],[15],[0],[13],[15],[10],[10],[14],[18],[1],[12],[1],[14],[5],[18],[9],[16],[11],[12],[16],[15],[10],[9],[3],[9],[14],[8],[1],[14],[0],[6],[3],[8],[15],[4],[4],[8],[8],[17],[16],[17],[15],[11],[18],[0],[11],[3],[1],[15],[18],[12],[10],[5],[8],[6],[18],[7],[7],[1],[16],[2],[1],[1],[6],[18],[1],[6],[14],[4],[6],[13],[4],[13],[3],[6],[10],[11],[7],[2],[5],[17],[12],[18],[18],[12],[18],[18],[16],[9],[3],[4],[15],[16],[10],[16],[15],[2],[11],[6],[3],[17],[3],[11],[4],[3],[18],[3],[7],[11],[5],[15],[14],[17],[4],[5],[16],[4],[3],[17],[9],[13],[16],[11],[6],[4],[3],[5],[8],[4],[12],[13],[17],[17],[10],[13],[11],[2],[17],[10],[18],[2],[9],[10],[1],[1],[3],[14],[17],[18],[14],[3],[14]],[[6],[9],[9],[5],[13],[5],[12],[0],[4],[13],[14],[10],[12],[13],[16],[11],[6],[0],[5],[17],[8],[15],[12],[7],[11],[10],[12],[9],[4],[16],[14],[9],[6],[14],[3],[3],[16],[0],[0],[2],[15],[7],[15],[5],[2],[8],[7],[12],[11],[3],[8],[14],[9],[16],[10],[5],[12],[3],[10],[1],[10],[17],[0],[12],[11],[6],[15],[1],[11],[9],[9],[10],[7],[7],[4],[16],[7],[0],[8],[17],[1],[1],[15],[16],[0],[5],[16],[3],[11],[12],[18],[6],[17],[9],[4],[13],[9],[4],[9],[18],[11],[3],[7],[10],[14],[12],[17],[4],[4],[11],[10],[13],[4],[16],[12],[1],[5],[0],[3],[2],[6],[11],[2],[17],[7],[12],[4],[17],[0],[18],[11],[13],[17],[6],[5],[12],[4],[3],[7],[2],[18],[10],[4],[17],[11],[10],[6],[7],[17],[5],[4],[15],[10],[2],[13],[13],[7],[5],[5],[2],[7],[15],[14],[3],[10],[1],[8],[11],[16],[7],[1],[7],[3],[17],[7],[18],[10],[2],[13],[16],[16],[5],[5],[17],[7],[10],[12],[14],[8],[9],[9],[8],[0],[10],[17],[11],[14],[0],[18],[11],[15],[8],[16],[1],[1],[14],[9],[0],[15],[12],[2],[5],[0],[12],[12],[12],[14],[1],[6],[8],[10],[5],[8],[5],[7],[2],[0],[1],[11],[9],[4],[10],[10],[16],[14],[6],[0],[4],[16],[0],[5],[0],[3],[13],[8],[1],[17],[17],[14],[9],[16],[1],[2],[9],[17],[17]],[[11],[5],[13],[2],[10],[9],[18],[8],[6],[13],[10],[7],[10],[12],[3],[0],[16],[12],[9],[11],[17],[11],[1],[8],[9],[13],[8],[8],[5],[3],[5],[2],[10],[5],[1],[0],[10],[10],[1],[10],[5],[15],[1],[10],[1],[17],[11],[7],[4],[2],[2],[17],[3],[6],[14],[18],[2],[18],[15],[8],[0],[12],[7],[1],[6],[5],[13],[14],[12],[3],[12],[15],[16],[12],[8],[3],[13],[14],[5],[3],[1],[0],[6],[12],[17],[9],[4],[3],[6],[2],[14],[4],[18],[1],[2],[0],[15],[7],[9],[1],[1],[16],[6],[7],[0],[5],[3],[8],[0],[9],[5],[7],[10],[7],[8],[2],[1],[8],[6],[14],[11],[2],[11],[9],[13],[18],[13],[10],[5],[0],[4],[6],[7],[14],[16],[4],[18],[2],[6],[7],[2],[18],[12],[9],[6],[3],[7],[6],[9],[5],[17],[15],[14],[12],[11],[17],[6],[1],[11],[5],[8],[2],[2],[13],[8],[7],[17],[6],[7],[16],[0],[10],[15],[11],[1],[6],[6],[14],[16],[4],[2],[5],[12],[7],[9],[8],[6],[12],[18],[10],[0],[15],[7],[2],[17],[0],[12],[3],[13],[0],[7],[1],[5],[5],[1],[17],[1],[18],[0],[1],[18],[13],[15],[14],[7],[3],[18],[2],[5],[12],[9],[15],[18],[2],[7],[17],[2],[2],[6],[14],[11],[17],[18],[16],[16],[16],[17],[18],[13],[1],[16],[7],[0],[17],[6],[18],[17],[0],[2],[12],[11],[14],[14],[8],[6],[12]],[[9],[2],[1],[2],[3],[3],[7],[5],[16],[2],[10],[14],[8],[3],[18],[0],[3],[17],[18],[14],[8],[18],[14],[13],[17],[13],[10],[4],[17],[16],[16],[0],[12],[12],[0],[2],[2],[15],[11],[9],[6],[7],[9],[5],[11],[7],[17],[14],[18],[15],[11],[1],[8],[15],[11],[6],[16],[13],[5],[18],[18],[14],[5],[2],[3],[17],[10],[12],[18],[8],[4],[12],[16],[2],[8],[5],[5],[15],[7],[9],[16],[0],[7],[0],[2],[0],[9],[16],[1],[16],[13],[2],[4],[10],[1],[2],[3],[1],[18],[17],[1],[7],[5],[15],[0],[18],[9],[17],[14],[1],[3],[18],[0],[14],[10],[13],[0],[7],[11],[16],[18],[16],[6],[18],[6],[14],[11],[11],[3],[8],[8],[1],[1],[8],[4],[13],[15],[9],[15],[4],[0],[6],[4],[11],[8],[2],[5],[13],[8],[4],[8],[0],[0],[10],[4],[14],[10],[17],[5],[16],[0],[11],[9],[2],[15],[10],[13],[6],[3],[11],[3],[0],[13],[8],[12],[17],[2],[14],[17],[0],[9],[6],[17],[4],[0],[10],[7],[15],[14],[13],[16],[0],[10],[9],[12],[16],[2],[8],[2],[7],[17],[3],[17],[1],[12],[16],[11],[1],[12],[18],[5],[15],[11],[2],[7],[6],[1],[16],[9],[13],[6],[4],[6],[5],[12],[7],[3],[10],[0],[10],[3],[2],[15],[7],[10],[15],[8],[3],[1],[8],[18],[12],[14],[10],[2],[18],[1],[11],[2],[10],[0],[14],[11],[18],[1],[3]],[[17],[3],[2],[9],[13],[7],[2],[13],[0],[10],[1],[10],[2],[4],[10],[2],[5],[6],[7],[18],[1],[16],[4],[15],[7],[11],[5],[16],[0],[10],[6],[7],[17],[11],[10],[9],[4],[8],[9],[11],[2],[8],[12],[17],[10],[5],[0],[14],[2],[7],[5],[3],[10],[13],[2],[13],[17],[0],[11],[13],[3],[2],[16],[14],[4],[10],[10],[18],[14],[10],[2],[1],[18],[2],[18],[14],[10],[4],[15],[5],[15],[1],[7],[14],[3],[2],[10],[4],[7],[17],[11],[3],[4],[0],[17],[16],[3],[17],[0],[3],[15],[9],[17],[12],[10],[15],[13],[2],[0],[4],[16],[14],[12],[9],[4],[12],[15],[6],[4],[10],[12],[17],[4],[10],[3],[6],[16],[9],[7],[18],[14],[8],[14],[10],[3],[3],[11],[13],[1],[6],[17],[12],[7],[14],[2],[14],[8],[14],[2],[5],[11],[14],[3],[2],[12],[5],[7],[6],[8],[3],[15],[16],[12],[15],[6],[13],[7],[5],[1],[2],[14],[4],[3],[13],[11],[9],[15],[16],[0],[1],[18],[13],[4],[15],[5],[16],[9],[3],[14],[0],[11],[11],[18],[9],[3],[15],[5],[4],[1],[6],[15],[10],[4],[8],[14],[6],[17],[6],[13],[10],[1],[7],[14],[0],[1],[5],[9],[14],[12],[14],[4],[14],[5],[9],[9],[2],[18],[16],[8],[2],[9],[3],[12],[15],[2],[3],[8],[12],[11],[9],[12],[0],[7],[12],[1],[10],[4],[1],[11],[17],[18],[17],[10],[5],[15],[1]],[[3],[16],[11],[10],[10],[17],[14],[13],[17],[18],[1],[2],[7],[18],[3],[13],[4],[6],[12],[11],[9],[15],[10],[12],[1],[14],[0],[16],[2],[16],[0],[3],[1],[18],[5],[12],[17],[6],[13],[8],[9],[14],[11],[11],[5],[4],[8],[0],[4],[0],[4],[17],[7],[17],[13],[7],[15],[10],[1],[11],[15],[13],[14],[1],[2],[9],[16],[16],[6],[3],[13],[7],[8],[5],[10],[18],[2],[11],[7],[18],[8],[8],[2],[17],[8],[0],[1],[17],[12],[15],[12],[11],[7],[5],[4],[12],[3],[4],[14],[4],[9],[18],[0],[16],[7],[1],[17],[2],[15],[5],[15],[2],[14],[14],[11],[6],[18],[14],[0],[15],[7],[10],[8],[1],[18],[7],[5],[18],[1],[11],[12],[6],[17],[13],[15],[12],[0],[8],[2],[15],[5],[3],[10],[3],[3],[11],[3],[16],[15],[7],[10],[13],[9],[8],[12],[11],[9],[9],[4],[18],[15],[1],[13],[7],[17],[17],[3],[15],[3],[8],[4],[17],[15],[4],[16],[18],[15],[9],[16],[15],[15],[15],[16],[3],[10],[16],[11],[4],[10],[3],[5],[15],[13],[7],[6],[13],[17],[18],[9],[13],[18],[4],[15],[10],[0],[17],[7],[8],[8],[9],[15],[12],[9],[8],[4],[13],[10],[10],[12],[1],[15],[6],[18],[8],[18],[6],[5],[16],[6],[13],[17],[10],[12],[5],[12],[2],[18],[10],[7],[2],[11],[12],[9],[7],[16],[12],[1],[15],[5],[12],[0],[5],[18],[6],[9],[6]],[[6],[12],[1],[16],[8],[9],[18],[18],[13],[10],[5],[5],[8],[6],[1],[18],[13],[4],[7],[4],[1],[2],[4],[14],[15],[4],[1],[13],[13],[6],[11],[18],[2],[5],[4],[1],[18],[6],[11],[16],[1],[7],[16],[7],[6],[18],[17],[13],[1],[10],[4],[11],[5],[8],[6],[15],[12],[12],[14],[17],[18],[7],[1],[5],[6],[8],[16],[1],[2],[3],[16],[5],[13],[8],[1],[18],[9],[8],[3],[18],[18],[5],[10],[8],[9],[15],[10],[9],[2],[18],[12],[18],[6],[2],[17],[16],[10],[1],[2],[17],[12],[8],[1],[1],[10],[16],[7],[7],[6],[8],[16],[9],[1],[13],[12],[6],[14],[6],[15],[0],[0],[7],[7],[8],[7],[16],[16],[6],[6],[17],[16],[1],[12],[11],[4],[1],[7],[10],[2],[8],[12],[18],[15],[8],[10],[6],[14],[3],[9],[10],[8],[6],[4],[12],[6],[4],[10],[13],[9],[15],[18],[10],[2],[13],[3],[5],[15],[12],[10],[3],[10],[16],[13],[11],[3],[15],[6],[13],[0],[4],[15],[17],[13],[4],[3],[8],[2],[17],[9],[13],[14],[7],[9],[17],[13],[6],[7],[6],[8],[3],[14],[11],[11],[7],[12],[3],[13],[4],[15],[11],[3],[14],[8],[5],[1],[2],[18],[6],[6],[18],[7],[17],[15],[15],[6],[16],[18],[5],[15],[16],[12],[2],[5],[15],[6],[17],[1],[13],[6],[11],[13],[17],[7],[5],[6],[7],[15],[17],[0],[15],[1],[2],[15],[15],[18],[4]],[[14],[17],[15],[0],[0],[8],[5],[17],[6],[5],[17],[9],[5],[15],[18],[4],[6],[15],[17],[0],[17],[15],[9],[4],[16],[17],[0],[9],[14],[2],[16],[15],[6],[12],[15],[9],[14],[13],[2],[7],[4],[6],[11],[18],[18],[15],[17],[3],[7],[12],[13],[0],[10],[13],[8],[10],[17],[14],[6],[8],[18],[4],[7],[6],[1],[11],[17],[17],[12],[1],[2],[1],[14],[11],[9],[17],[6],[7],[17],[0],[7],[16],[10],[11],[6],[1],[5],[14],[8],[10],[14],[3],[8],[5],[17],[0],[12],[5],[18],[7],[17],[2],[4],[17],[5],[12],[5],[18],[13],[12],[14],[16],[2],[7],[7],[15],[8],[6],[1],[7],[3],[12],[17],[10],[1],[12],[5],[7],[7],[10],[9],[11],[1],[2],[6],[3],[16],[8],[17],[8],[14],[9],[17],[2],[1],[8],[11],[12],[15],[9],[18],[10],[10],[14],[12],[0],[11],[6],[17],[8],[4],[4],[1],[8],[15],[8],[3],[1],[14],[17],[6],[1],[3],[10],[4],[0],[12],[15],[4],[17],[13],[6],[2],[10],[2],[11],[15],[0],[13],[18],[0],[1],[12],[10],[14],[18],[10],[6],[13],[12],[14],[12],[4],[8],[2],[3],[0],[2],[11],[17],[14],[12],[9],[3],[10],[4],[13],[14],[5],[6],[11],[5],[15],[11],[2],[9],[11],[10],[9],[0],[16],[4],[9],[17],[6],[15],[2],[16],[16],[5],[0],[13],[6],[14],[8],[7],[6],[18],[16],[7],[10],[8],[0],[5],[8],[1]],[[6],[10],[9],[6],[12],[2],[9],[17],[1],[5],[13],[10],[18],[7],[12],[5],[12],[12],[16],[11],[3],[2],[17],[12],[1],[8],[12],[18],[9],[0],[4],[2],[16],[8],[10],[18],[12],[16],[0],[14],[17],[14],[6],[0],[0],[15],[7],[18],[16],[7],[10],[11],[15],[12],[4],[3],[16],[13],[11],[7],[7],[9],[10],[15],[18],[7],[1],[0],[15],[12],[18],[16],[9],[17],[16],[6],[6],[16],[3],[2],[15],[14],[14],[10],[18],[6],[2],[2],[11],[3],[17],[5],[8],[1],[8],[5],[3],[18],[0],[13],[5],[4],[6],[12],[1],[18],[6],[4],[10],[2],[14],[15],[7],[4],[7],[9],[6],[3],[10],[18],[17],[17],[11],[5],[13],[16],[5],[12],[5],[12],[2],[16],[9],[5],[6],[1],[15],[13],[3],[14],[9],[16],[18],[2],[16],[2],[15],[17],[8],[13],[14],[9],[5],[9],[7],[12],[10],[9],[15],[9],[4],[17],[2],[17],[6],[13],[0],[7],[0],[13],[4],[11],[2],[4],[17],[9],[12],[9],[12],[18],[18],[8],[1],[16],[8],[15],[13],[6],[1],[18],[3],[8],[17],[15],[14],[10],[14],[12],[17],[10],[4],[7],[1],[15],[17],[5],[12],[14],[2],[15],[6],[11],[11],[13],[12],[16],[10],[13],[18],[16],[16],[9],[8],[12],[11],[3],[8],[12],[11],[4],[10],[2],[2],[14],[16],[18],[6],[11],[17],[5],[15],[3],[8],[11],[7],[4],[0],[8],[15],[8],[1],[12],[18],[0],[14],[16]],[[2],[7],[14],[18],[14],[12],[1],[18],[14],[12],[16],[6],[9],[10],[0],[13],[8],[3],[6],[0],[14],[6],[17],[16],[15],[15],[4],[13],[14],[9],[8],[17],[6],[11],[3],[13],[10],[18],[9],[10],[4],[3],[17],[4],[7],[5],[10],[9],[14],[6],[4],[11],[4],[10],[13],[11],[14],[6],[14],[15],[7],[0],[4],[6],[17],[2],[13],[16],[10],[12],[0],[12],[10],[7],[6],[4],[12],[16],[14],[1],[11],[14],[18],[3],[6],[3],[14],[18],[2],[1],[10],[6],[4],[8],[16],[5],[1],[10],[14],[11],[10],[13],[11],[8],[5],[5],[4],[1],[18],[4],[11],[2],[16],[6],[1],[2],[13],[5],[12],[10],[3],[7],[3],[18],[5],[8],[10],[15],[3],[18],[14],[1],[9],[8],[13],[13],[14],[3],[17],[6],[16],[4],[17],[8],[7],[15],[14],[18],[0],[5],[13],[10],[4],[14],[8],[0],[6],[14],[8],[8],[17],[5],[6],[16],[12],[3],[18],[15],[11],[1],[7],[11],[2],[14],[2],[8],[4],[14],[8],[10],[3],[7],[6],[15],[1],[5],[18],[18],[17],[13],[8],[2],[3],[2],[6],[4],[5],[7],[16],[10],[0],[8],[11],[2],[14],[6],[15],[6],[17],[14],[7],[11],[2],[14],[5],[16],[5],[5],[6],[4],[3],[6],[14],[18],[2],[8],[9],[3],[6],[5],[9],[10],[5],[6],[16],[9],[8],[17],[16],[12],[14],[14],[14],[11],[16],[2],[4],[15],[9],[9],[16],[13],[16],[15],[16],[11]],[[10],[3],[18],[6],[1],[18],[6],[12],[15],[18],[9],[2],[4],[10],[6],[15],[1],[12],[17],[3],[12],[17],[15],[1],[3],[15],[16],[5],[13],[18],[16],[1],[1],[8],[18],[8],[1],[8],[12],[2],[17],[12],[4],[12],[12],[16],[0],[10],[13],[0],[6],[0],[6],[17],[18],[17],[12],[0],[1],[9],[18],[11],[13],[0],[6],[18],[14],[2],[9],[9],[8],[2],[3],[16],[15],[14],[4],[9],[17],[13],[6],[2],[8],[2],[7],[5],[12],[13],[2],[16],[2],[7],[9],[7],[6],[6],[5],[8],[9],[6],[5],[14],[18],[5],[10],[1],[14],[10],[0],[13],[14],[11],[13],[16],[12],[5],[5],[0],[7],[1],[8],[4],[5],[12],[2],[1],[16],[4],[7],[17],[10],[5],[6],[12],[4],[13],[2],[4],[6],[6],[15],[4],[0],[13],[5],[12],[9],[4],[12],[9],[10],[3],[11],[4],[8],[16],[6],[0],[17],[11],[17],[3],[5],[9],[17],[16],[5],[5],[15],[10],[4],[4],[6],[0],[14],[16],[5],[12],[12],[3],[13],[8],[10],[5],[1],[14],[5],[16],[5],[13],[2],[5],[8],[6],[17],[12],[6],[4],[14],[4],[15],[2],[11],[11],[10],[9],[8],[16],[12],[15],[7],[15],[3],[1],[15],[16],[1],[10],[8],[2],[17],[14],[13],[13],[13],[7],[13],[3],[10],[17],[7],[1],[15],[4],[7],[11],[11],[5],[18],[5],[9],[8],[18],[10],[6],[15],[2],[11],[10],[8],[13],[12],[9],[4],[7],[18]],[[11],[8],[9],[6],[14],[17],[6],[2],[15],[0],[12],[5],[13],[7],[7],[1],[12],[13],[1],[7],[8],[3],[18],[18],[17],[4],[16],[12],[12],[18],[13],[9],[7],[7],[16],[3],[16],[6],[6],[12],[17],[17],[18],[15],[1],[15],[13],[14],[5],[7],[8],[11],[1],[10],[16],[5],[13],[10],[2],[6],[6],[8],[17],[2],[6],[10],[11],[18],[10],[4],[10],[5],[5],[16],[8],[6],[4],[2],[3],[6],[4],[7],[14],[18],[14],[7],[13],[4],[0],[17],[11],[15],[13],[6],[14],[11],[2],[18],[18],[15],[1],[18],[0],[18],[9],[9],[17],[15],[1],[7],[6],[17],[17],[11],[15],[14],[17],[1],[1],[16],[5],[14],[17],[14],[10],[9],[5],[3],[16],[3],[7],[17],[3],[8],[10],[18],[5],[17],[8],[9],[10],[5],[17],[17],[6],[5],[9],[11],[14],[16],[14],[2],[3],[6],[1],[0],[9],[0],[17],[1],[13],[3],[2],[9],[12],[15],[13],[13],[10],[4],[13],[7],[4],[1],[14],[17],[17],[0],[16],[8],[17],[14],[12],[0],[0],[2],[1],[17],[16],[9],[3],[11],[0],[9],[5],[8],[12],[4],[9],[15],[5],[1],[14],[2],[1],[4],[18],[7],[0],[5],[5],[1],[16],[16],[18],[13],[2],[0],[2],[1],[5],[16],[11],[4],[14],[8],[10],[16],[10],[0],[7],[13],[15],[17],[7],[4],[7],[7],[15],[7],[0],[6],[13],[9],[9],[5],[0],[12],[17],[7],[8],[8],[17],[10],[2],[10]],[[15],[4],[18],[7],[0],[13],[2],[15],[14],[5],[2],[15],[18],[16],[13],[3],[13],[6],[13],[12],[13],[14],[16],[12],[14],[6],[16],[18],[12],[8],[10],[5],[3],[6],[3],[16],[12],[1],[1],[13],[14],[7],[18],[1],[16],[16],[11],[6],[15],[17],[8],[1],[4],[4],[12],[6],[15],[14],[4],[7],[11],[17],[15],[8],[15],[7],[1],[15],[12],[6],[8],[10],[9],[1],[8],[1],[12],[12],[1],[18],[17],[2],[16],[8],[11],[18],[3],[1],[11],[16],[16],[15],[10],[11],[9],[4],[13],[1],[18],[3],[12],[11],[12],[3],[1],[13],[12],[8],[0],[12],[2],[5],[1],[6],[5],[9],[15],[11],[4],[0],[13],[15],[0],[3],[1],[17],[0],[0],[3],[10],[6],[4],[7],[9],[12],[1],[4],[0],[7],[5],[6],[11],[12],[15],[3],[7],[13],[9],[16],[17],[1],[6],[1],[0],[18],[9],[4],[15],[1],[13],[17],[16],[18],[9],[14],[8],[13],[6],[13],[8],[9],[6],[16],[13],[2],[7],[12],[16],[16],[8],[2],[13],[10],[4],[12],[1],[8],[1],[3],[0],[7],[0],[7],[3],[14],[12],[10],[18],[2],[2],[0],[18],[17],[13],[9],[14],[8],[2],[15],[2],[9],[2],[4],[0],[17],[10],[3],[15],[7],[0],[18],[1],[4],[17],[17],[17],[0],[11],[0],[11],[4],[2],[5],[1],[11],[2],[1],[9],[16],[12],[2],[0],[8],[8],[9],[4],[2],[1],[17],[10],[8],[0],[8],[10],[6],[3]]]
ZW = 279
def setup_inputs(rng):
    return {"z": rng.standard_normal((N, 128, ZW), dtype=np.float32)}
def reference(z):
    y = np.zeros((N, 128, T), np.float64)
    fill = [0] * N
    for r in range(N):
        for t in range(T):
            for e in ROUTE[r][t]:
                y[r][:, t] += z[e][:, fill[e]].astype(np.float64)
                fill[e] += 1
    return {"y": y.astype(z.dtype)}

@@ -1,0 +1,150 @@
+import comms_topo
+
+SCRATCH = {
+    "zs": ("sbuf", [128, 279], "float32"),
+    "land": ("sbuf", [128, 256], "float32"),
+    "ybuf": ("sbuf", [128, 256], "float32"),
+}
+SEMAPHORES = ["ld", "hand", "arr", "sent", "scg", "sc", "st"]
+
+_PLAN = {}
+
+
+def _bits(m):
+    n = 0
+    while m:
+        n += m & 1
+        m >>= 1
+    return n
+
+
+def _plan(T, topo):
+    if "p" in _PLAN:
+        return _PLAN["p"]
+    route, cores = T.tables["ROUTE"], list(T.cores)
+    n, nt = len(cores), len(route[0])
+    cnt = [[0] * n for _ in range(n)]
+    for r in range(n):
+        for t in range(nt):
+            cnt[route[r][t][0]][r] += 1
+    zoff = [[sum(cnt[e][:r]) for r in range(n + 1)] for e in range(n)]
+
+    g3, g2 = cores[15] - 2, cores[18] - 2
+    rack1 = list(range(16)) + [18]
+    gate = {16: g3, 17: g2}
+    via = {16: rack1, 17: list(range(16))}
+
+    loff, gath = [], {}
+    for r in range(n):
+        order = [e for e in via.get(r, []) if e != r] + [e for e in range(n) if e != r and e not in via.get(r, [])]
+        o, d = 0, {}
+        for e in order:
+            d[e] = o
+            o += cnt[e][r]
+        loff.append(d)
+        if r in via:
+            gath[r] = sum(cnt[e][r] for e in via[r])
+
+    sends = {}
+    expect = {}
+
+    def put(stage, src, dst, dbuf, dcol, sbuf, scol, w, sem):
+        sends.setdefault(src, []).append((stage, dst, dbuf, dcol, sbuf, scol, w, sem))
+        expect[(dst, sem)] = expect.get((dst, sem), 0) + _bits(topo.mask(src, dst))
+
+    for e in range(n):
+        c = cores[e]
+        far, near = [], []
+        for r in range(n):
+            if r == e:
+                continue
+            if e in gate:
+                (far if r in via[e] else near).append((r, cores[r]))
+            else:
+                tgt = gate[r] if (r in gate and e in via[r]) else cores[r]
+                (near if topo.may_write(c, tgt) else far).append((r, tgt))
+        proxy = gate.get(e, c + 2)
+        rs = [r for r, _ in far]
+        if e in gate:
+            spans, k = [], 0
+            while k < len(rs):
+                j = k
+                while j + 1 < len(rs) and rs[j + 1] == rs[j] + 1:
+                    j += 1
+                spans.append((zoff[e][rs[k]], zoff[e][rs[j] + 1]))
+                k = j + 1
+        else:
+            spans = [(zoff[e][rs[0]], zoff[e][rs[-1] + 1])]
+        for a, b in spans:
+            put(0, c, proxy, "zs", a, "zs", a, b - a, "hand")
+        for who, lst in ((c, near), (proxy, far)):
+            for r, tgt in sorted(lst, key=lambda x: (x[1] == cores[x[0]], x[0])):
+                put(1, who, tgt, "land", loff[r][e], "zs", zoff[e][r], cnt[e][r], "arr")
+    for r in gate:
+        put(2, gate[r], cores[r], "land", 0, "land", 0, gath[r], "arr")
+
+    scat = []
+    for r in range(n):
+        seen, lst = [0] * n, []
+        for t in range(nt):
+            e = route[r][t][0]
+            buf, col = ("zs", zoff[e][r] + seen[e]) if e == r else ("land", loff[r][e] + seen[e])
+            seen[e] += 1
+            if lst and lst[-1][2] == buf and lst[-1][3] + lst[-1][1] == col and route[r][t - 1][0] == e:
+                lst[-1] = (lst[-1][0], lst[-1][1] + 1, buf, lst[-1][3])
+            else:
+                lst.append((t, 1, buf, col))
+        scat.append(lst)
+    p = {"sends": sends, "expect": expect, "scat": scat, "used": [zoff[e][n] for e in range(n)]}
+    _PLAN["p"] = p
+    return p
+
+
+def rank_program(g, core, T, topo):
+    p = _plan(T, topo)
+    rank = T.rank_of(core)
+    mine = p["sends"].get(core, [])
+    if rank is None and not mine:
+        return
+    sent = [0]
+
+    def issue(stage):
+        for st, dst, dbuf, dcol, sbuf, scol, w, sem in mine:
+            if st != stage:
+                continue
+            rid, pid = topo.addr(dst, core)
+            m = topo.mask(core, dst)
+            g.remote_dma(out_ap=T[dbuf][:, dcol:dcol + w], in_ap=T[sbuf][:, scol:scol + w], remote_sem=T.sem[sem],
+                         local_sem=T.sem.sent, pid=pid, routing_id=rid, dma_engine_mask=m)
+            sent[0] += _bits(m)
+
+    arr = p["expect"].get((core, "arr"), 0)
+    if rank is None:
+        g.wait_ge(T.sem.hand, p["expect"][(core, "hand")])
+        issue(1)
+        if arr:
+            g.wait_ge(T.sem.arr, arr)
+            issue(2)
+        g.wait_ge(T.sem.sent, sent[0])
+        return
+
+    w = p["used"][rank]
+    g.sync.dma_start(T.zs[:, 0:w], T.z[:, 0:w]).then_inc(T.sem.ld, 16)
+    g.wait_ge(T.sem.ld, 16)
+    issue(0)
+    issue(1)
+    qs = [(g, T.sem.scg), (g.sync, T.sem.sc), (g.scalar, T.sem.sc)]
+    for q, _ in qs:
+        q.wait_ge(T.sem.arr, arr)
+    g.sync.wait_ge(T.sem.ld, 16)
+    g.scalar.wait_ge(T.sem.ld, 16)
+    n = [0, 0, 0]
+    for k, (t, wd, buf, col) in enumerate(p["scat"][rank]):
+        q, s = qs[k % 3]
+        q.dma_start(T.ybuf[:, t:t + wd], T[buf][:, col:col + wd]).then_inc(s, 16)
+        n[k % 3] += 16
+    g.wait_ge(T.sem.scg, n[0])
+    g.wait_ge(T.sem.sc, n[1] + n[2])
+    g.dma_start(T.y[:, :], T.ybuf[:, :]).then_inc(T.sem.st, 16)
+    g.wait_ge(T.sem.st, 16)
+    g.wait_ge(T.sem.sent, sent[0])

@@ -1,11 +1,12 @@
 import comms_topo
+from concourse.bass import DstId, RemoteDMATransfer
 
 SCRATCH = {
     "zs": ("sbuf", [128, 279], "float32"),
-    "land": ("sbuf", [128, 256], "float32"),
+    "land": ("sbuf", [128, 64], "float32"),
     "ybuf": ("sbuf", [128, 256], "float32"),
 }
-SEMAPHORES = ["ld", "hand", "arr", "sent", "scg", "sc", "st"]
+SEMAPHORES = ["ld", "hand", "a1", "a2", "col", "sent", "locg", "loc", "st"]
 
 _PLAN = {}
 
@@ -18,10 +19,18 @@ def _bits(m):
     return n
 
 
-def _plan(T, topo):
-    if "p" in _PLAN:
-        return _PLAN["p"]
-    route, cores = T.tables["ROUTE"], list(T.cores)
+def _runs(rs):
+    out = []
+    for r in rs:
+        if out and out[-1][1] + 1 == r:
+            out[-1][1] = r
+        else:
+            out.append([r, r])
+    return out
+
+
+def make_plan(tables, cores, topo):
+    route = tables["ROUTE"]
     n, nt = len(cores), len(route[0])
     cnt = [[0] * n for _ in range(n)]
     for r in range(n):
@@ -29,122 +38,188 @@ def _plan(T, topo):
             cnt[route[r][t][0]][r] += 1
     zoff = [[sum(cnt[e][:r]) for r in range(n + 1)] for e in range(n)]
 
-    g3, g2 = cores[15] - 2, cores[18] - 2
-    rack1 = list(range(16)) + [18]
-    gate = {16: g3, 17: g2}
-    via = {16: rack1, 17: list(range(16))}
+    def on(c, k):
+        return c - c % 8 + k
 
-    loff, gath = [], {}
-    for r in range(n):
-        order = [e for e in via.get(r, []) if e != r] + [e for e in range(n) if e != r and e not in via.get(r, [])]
-        o, d = 0, {}
-        for e in order:
-            d[e] = o
-            o += cnt[e][r]
-        loff.append(d)
-        if r in via:
-            gath[r] = sum(cnt[e][r] for e in via[r])
+    def across(c):
+        return (3 - topo.host(c)) * 128 + c % 128
 
-    sends = {}
+    ring = [i for i in range(n) if topo.rack(topo.host(cores[i])) == 1]
+    far = [i for i in range(n) if i not in ring]
+    chip_rank = {on(cores[i], 0): i for i in range(n)}
+
+    blocks = {}
     expect = {}
+    top = {}
+    hold = {}
 
     def put(stage, src, dst, dbuf, dcol, sbuf, scol, w, sem):
-        sends.setdefault(src, []).append((stage, dst, dbuf, dcol, sbuf, scol, w, sem))
+        blocks.setdefault(src, {}).setdefault(stage, []).append((dst, dbuf, dcol, sbuf, scol, w, sem))
         expect[(dst, sem)] = expect.get((dst, sem), 0) + _bits(topo.mask(src, dst))
+
+    def room(c, w):
+        a = top.get(c, 0)
+        top[c] = a + w
+        return a
+
+    def by_cable_columns(e, r):
+        return e in far and r in ring and on(across(cores[r]), 0) not in chip_rank
+
+    recv = []
+    for r in range(n):
+        load = {k: 0 for k in range(8)}
+        load[4], load[6], load[2] = cnt[r][r] + 6, 8, 8
+        d = {}
+        for e in sorted([e for e in range(n) if e != r and not by_cable_columns(e, r)], key=lambda e: (-cnt[e][r], e)):
+            k = min(load, key=lambda k: (load[k], k))
+            load[k] += cnt[e][r]
+            d[e] = on(cores[r], k)
+        recv.append(d)
+
+    def final(stage, src, e, r, sbuf, scol):
+        dst = recv[r][e]
+        a = room(dst, cnt[e][r])
+        put(stage, src, dst, "land", a, sbuf, scol, cnt[e][r], "a2")
+        hold[(e, r)] = (dst, "land", a)
+
+    def pair(e, keep, go):
+        lo = min(keep, go)
+        dst = recv[keep][e]
+        a = room(dst, cnt[e][keep] + cnt[e][go])
+        put(0, cores[e], dst, "land", a, "zs", zoff[e][lo], cnt[e][keep] + cnt[e][go], "a1")
+        hold[(e, keep)] = (dst, "land", a + zoff[e][keep] - zoff[e][lo])
+        final(2, dst, e, go, "land", a + zoff[e][go] - zoff[e][lo])
 
     for e in range(n):
         c = cores[e]
-        far, near = [], []
-        for r in range(n):
-            if r == e:
-                continue
-            if e in gate:
-                (far if r in via[e] else near).append((r, cores[r]))
-            else:
-                tgt = gate[r] if (r in gate and e in via[r]) else cores[r]
-                (near if topo.may_write(c, tgt) else far).append((r, tgt))
-        proxy = gate.get(e, c + 2)
-        rs = [r for r, _ in far]
-        if e in gate:
-            spans, k = [], 0
-            while k < len(rs):
-                j = k
-                while j + 1 < len(rs) and rs[j + 1] == rs[j] + 1:
-                    j += 1
-                spans.append((zoff[e][rs[k]], zoff[e][rs[j] + 1]))
-                k = j + 1
+        hold[(e, e)] = (c, "zs", zoff[e][e])
+        if e in ring:
+            i, m = ring.index(e), len(ring)
+            halves = [[ring[(i + j) % m] for j in range(1, 1 + m // 2)], [ring[(i + j) % m] for j in range(1 + m // 2, m)]]
         else:
-            spans = [(zoff[e][rs[0]], zoff[e][rs[-1] + 1])]
-        for a, b in spans:
-            put(0, c, proxy, "zs", a, "zs", a, b - a, "hand")
-        for who, lst in ((c, near), (proxy, far)):
-            for r, tgt in sorted(lst, key=lambda x: (x[1] == cores[x[0]], x[0])):
-                put(1, who, tgt, "land", loff[r][e], "zs", zoff[e][r], cnt[e][r], "arr")
-    for r in gate:
-        put(2, gate[r], cores[r], "land", 0, "land", 0, gath[r], "arr")
+            ks = [r for r in ring if by_cable_columns(e, r)]
+            halves = [ks[:(len(ks) + 1) // 2], ks[(len(ks) + 1) // 2:]]
+        for k, half in ((6, halves[0]), (2, halves[1])):
+            h = on(c, k)
+            for a, b in _runs(sorted(half)):
+                put(0, c, h, "zs", zoff[e][a], "zs", zoff[e][a], zoff[e][b + 1] - zoff[e][a], "hand")
+            for r in half:
+                if e in ring:
+                    final(1, h, e, r, "zs", zoff[e][r])
+                else:
+                    dst = on(across(cores[r]), 0 if e == far[0] else 4)
+                    a = room(dst, cnt[e][r])
+                    put(1, h, dst, "land", a, "zs", zoff[e][r], cnt[e][r], "a2")
+                    hold[(e, r)] = (dst, "land", a)
+        if e in ring:
+            door = on(across(c), 0)
+            if door in chip_rank:
+                q = chip_rank[door]
+                pair(e, q, far[1] if q == far[0] else far[0])
+            else:
+                dst = door + (6 if (topo.chip(c) // 2) % 2 == 0 else 2)
+                w = cnt[e][far[0]] + cnt[e][far[1]]
+                a = room(dst, w)
+                put(0, c, dst, "land", a, "zs", zoff[e][far[0]], w, "a1")
+                for r in far:
+                    final(2, dst, e, r, "land", a + zoff[e][r] - zoff[e][far[0]])
+        else:
+            o = far[1] if e == far[0] else far[0]
+            final(0, c, e, chip_rank[on(across(c), 0)], "zs", zoff[e][chip_rank[on(across(c), 0)]])
+            pair(e, o, chip_rank[on(across(cores[o]), 0)])
 
-    scat = []
+    jobs = {}
     for r in range(n):
-        seen, lst = [0] * n, []
+        seen = [0] * n
         for t in range(nt):
             e = route[r][t][0]
-            buf, col = ("zs", zoff[e][r] + seen[e]) if e == r else ("land", loff[r][e] + seen[e])
+            c, buf, col = hold[(e, r)]
+            col += seen[e]
             seen[e] += 1
-            if lst and lst[-1][2] == buf and lst[-1][3] + lst[-1][1] == col and route[r][t - 1][0] == e:
+            lst = jobs.setdefault((c, r), [])
+            if lst and t and route[r][t - 1][0] == e:
                 lst[-1] = (lst[-1][0], lst[-1][1] + 1, buf, lst[-1][3])
             else:
                 lst.append((t, 1, buf, col))
-        scat.append(lst)
-    p = {"sends": sends, "expect": expect, "scat": scat, "used": [zoff[e][n] for e in range(n)]}
-    _PLAN["p"] = p
-    return p
+    cols, copies = {}, {}
+    for (c, r), lst in sorted(jobs.items()):
+        if c == cores[r]:
+            copies[r] = lst
+            continue
+        cap = _bits(topo.mask(c, cores[r]))
+        calls = cols.setdefault(c, (cores[r], []))[1]
+        for w in sorted(set(x[1] for x in lst)):
+            same = [x for x in lst if x[1] == w]
+            i = 0
+            while i < len(same):
+                m = min(cap, len(same) - i)
+                per = 1
+                while per * 2 * m <= cap:
+                    per *= 2
+                calls.append([(((1 << per) - 1) << (j * per),) + same[i + j] for j in range(m)])
+                expect[(cores[r], "col")] = expect.get((cores[r], "col"), 0) + per * m
+                i += m
+    return {"blocks": blocks, "expect": expect, "cols": cols, "copies": copies, "top": top,
+            "used": [zoff[e][n] for e in range(n)]}
 
 
 def rank_program(g, core, T, topo):
-    p = _plan(T, topo)
+    if "p" not in _PLAN:
+        _PLAN["p"] = make_plan(T.tables, list(T.cores), topo)
+    p = _PLAN["p"]
     rank = T.rank_of(core)
-    mine = p["sends"].get(core, [])
-    if rank is None and not mine:
+    mine = p["blocks"].get(core, {})
+    if rank is None and not mine and core not in p["cols"]:
         return
     sent = [0]
 
+    def need(sem):
+        return p["expect"].get((core, sem), 0)
+
     def issue(stage):
-        for st, dst, dbuf, dcol, sbuf, scol, w, sem in mine:
-            if st != stage:
-                continue
+        for dst, dbuf, dcol, sbuf, scol, w, sem in mine.get(stage, []):
             rid, pid = topo.addr(dst, core)
             m = topo.mask(core, dst)
             g.remote_dma(out_ap=T[dbuf][:, dcol:dcol + w], in_ap=T[sbuf][:, scol:scol + w], remote_sem=T.sem[sem],
                          local_sem=T.sem.sent, pid=pid, routing_id=rid, dma_engine_mask=m)
             sent[0] += _bits(m)
 
-    arr = p["expect"].get((core, "arr"), 0)
-    if rank is None:
-        g.wait_ge(T.sem.hand, p["expect"][(core, "hand")])
+    if rank is not None:
+        w = p["used"][rank]
+        g.sync.dma_start(T.zs[:, 0:w], T.z[:, 0:w]).then_inc(T.sem.ld, 16)
+        g.wait_ge(T.sem.ld, 16)
+        issue(0)
+    if need("hand"):
+        g.wait_ge(T.sem.hand, need("hand"))
         issue(1)
-        if arr:
-            g.wait_ge(T.sem.arr, arr)
-            issue(2)
-        g.wait_ge(T.sem.sent, sent[0])
-        return
-
-    w = p["used"][rank]
-    g.sync.dma_start(T.zs[:, 0:w], T.z[:, 0:w]).then_inc(T.sem.ld, 16)
-    g.wait_ge(T.sem.ld, 16)
-    issue(0)
-    issue(1)
-    qs = [(g, T.sem.scg), (g.sync, T.sem.sc), (g.scalar, T.sem.sc)]
-    for q, _ in qs:
-        q.wait_ge(T.sem.arr, arr)
-    g.sync.wait_ge(T.sem.ld, 16)
-    g.scalar.wait_ge(T.sem.ld, 16)
-    n = [0, 0, 0]
-    for k, (t, wd, buf, col) in enumerate(p["scat"][rank]):
-        q, s = qs[k % 3]
-        q.dma_start(T.ybuf[:, t:t + wd], T[buf][:, col:col + wd]).then_inc(s, 16)
-        n[k % 3] += 16
-    g.wait_ge(T.sem.scg, n[0])
-    g.wait_ge(T.sem.sc, n[1] + n[2])
-    g.dma_start(T.y[:, :], T.ybuf[:, :]).then_inc(T.sem.st, 16)
-    g.wait_ge(T.sem.st, 16)
+    if need("a1"):
+        g.wait_ge(T.sem.a1, need("a1"))
+        issue(2)
+    if need("a2"):
+        g.wait_ge(T.sem.a2, need("a2"))
+    if core in p["cols"]:
+        dst, calls = p["cols"][core]
+        rid, pid = topo.addr(dst, core)
+        for call in calls:
+            g.remote_dma_fused([RemoteDMATransfer(dst_ids=[DstId(rid=rid, pnc=pid)], dma_engine_mask=m, remote_sem=T.sem.col,
+                                                  src=T[buf][:, col:col + w], dst=T.ybuf[:, t:t + w])
+                                for m, t, w, buf, col in call], local_sem=T.sem.sent)
+            sent[0] += sum(_bits(x[0]) for x in call)
+    if rank is not None:
+        for q in (g.sync, g.scalar):
+            q.wait_ge(T.sem.ld, 16)
+            for s in ("a1", "a2"):
+                if need(s):
+                    q.wait_ge(T.sem[s], need(s))
+        qs = [(g.sync, T.sem.loc), (g.scalar, T.sem.loc), (g, T.sem.locg)]
+        done = [0, 0, 0]
+        for k, (t, w, buf, col) in enumerate(p["copies"][rank]):
+            q, s = qs[k % 3]
+            q.dma_start(T.ybuf[:, t:t + w], T[buf][:, col:col + w]).then_inc(s, 16)
+            done[k % 3] += 16
+        g.wait_ge(T.sem.locg, done[2])
+        g.wait_ge(T.sem.loc, done[0] + done[1])
+        g.wait_ge(T.sem.col, need("col"))
+        g.dma_start(T.y[:, :], T.ybuf[:, :]).then_inc(T.sem.st, 16)
+        g.wait_ge(T.sem.st, 16)
     g.wait_ge(T.sem.sent, sent[0])

@@ -3,7 +3,7 @@ from concourse.bass import DstId, RemoteDMATransfer
 
 SCRATCH = {
     "zs": ("sbuf", [128, 279], "float32"),
-    "land": ("sbuf", [128, 64], "float32"),
+    "land": ("sbuf", [128, 52], "float32"),
     "ybuf": ("sbuf", [128, 256], "float32"),
 }
 SEMAPHORES = ["ld", "hand", "a1", "a2", "col", "sent", "locg", "loc", "st"]
@@ -29,13 +29,46 @@ def _runs(rs):
     return out
 
 
+def _better(size, where, load):
+    hi = max(load, key=lambda k: (load[k], -k))
+    for a in sorted(e for e in where if where[e] == hi):
+        for k in sorted(load):
+            if k != hi:
+                for b in [None] + sorted(e for e in where if where[e] == k):
+                    d = size[a] - (size[b] if b is not None else 0)
+                    if d > 0 and load[k] + d < load[hi]:
+                        return a, b, hi, k, d
+    return None
+
+
+def _share(size, load):
+    where = {}
+    for e in sorted(size, key=lambda e: (-size[e], e)):
+        k = min(load, key=lambda k: (load[k], k))
+        load[k] += size[e]
+        where[e] = k
+    mv = _better(size, where, load)
+    while mv:
+        a, b, hi, k, d = mv
+        where[a] = k
+        if b is not None:
+            where[b] = hi
+        load[hi] -= d
+        load[k] += d
+        mv = _better(size, where, load)
+    return where
+
+
 def make_plan(tables, cores, topo):
     route = tables["ROUTE"]
     n, nt = len(cores), len(route[0])
     cnt = [[0] * n for _ in range(n)]
+    wide = [[0] * n for _ in range(n)]
     for r in range(n):
         for t in range(nt):
             cnt[route[r][t][0]][r] += 1
+            if t == 0 or route[r][t - 1][0] != route[r][t][0]:
+                wide[route[r][t][0]][r] += 1
     zoff = [[sum(cnt[e][:r]) for r in range(n + 1)] for e in range(n)]
 
     def on(c, k):
@@ -44,9 +77,13 @@ def make_plan(tables, cores, topo):
     def across(c):
         return (3 - topo.host(c)) * 128 + c % 128
 
+    def beside(c):
+        return (topo.host(c) ^ 1) * 128 + c % 128
+
     ring = [i for i in range(n) if topo.rack(topo.host(cores[i])) == 1]
     far = [i for i in range(n) if i not in ring]
-    chip_rank = {on(cores[i], 0): i for i in range(n)}
+    at = {cores[i]: i for i in range(n)}
+    corner = [i for i in range(n) if across(cores[i]) in at]
 
     blocks = {}
     expect = {}
@@ -62,19 +99,25 @@ def make_plan(tables, cores, topo):
         top[c] = a + w
         return a
 
-    def by_cable_columns(e, r):
-        return e in far and r in ring and on(across(cores[r]), 0) not in chip_rank
+    halves = []
+    for e in range(n):
+        if e in ring:
+            i, m = ring.index(e), len(ring)
+            rs = [ring[(i + j) % m] for j in range(1, m)]
+            if e in corner:
+                rs.remove(at[beside(cores[e])])
+        else:
+            rs = [r for r in ring if r not in corner]
+        halves.append([rs[:(len(rs) + 1) // 2], rs[(len(rs) + 1) // 2:]])
 
     recv = []
     for r in range(n):
         load = {k: 0 for k in range(8)}
-        load[4], load[6], load[2] = cnt[r][r] + 6, 8, 8
-        d = {}
-        for e in sorted([e for e in range(n) if e != r and not by_cable_columns(e, r)], key=lambda e: (-cnt[e][r], e)):
-            k = min(load, key=lambda k: (load[k], k))
-            load[k] += cnt[e][r]
-            d[e] = on(cores[r], k)
-        recv.append(d)
+        load[4] = wide[r][r] + 2 + sum(len(_runs(sorted(h))) for h in halves[r]) + (2 if r in corner else 1)
+        load[6], load[2] = len(halves[r][0]), len(halves[r][1])
+        size = {e: wide[e][r] + (1 if e in corner and at[beside(cores[e])] == r else 0)
+                for e in range(n) if e != r and not (e in far and r not in corner)}
+        recv.append({e: on(cores[r], k) for e, k in _share(size, load).items()})
 
     def final(stage, src, e, r, sbuf, scol):
         dst = recv[r][e]
@@ -82,24 +125,11 @@ def make_plan(tables, cores, topo):
         put(stage, src, dst, "land", a, sbuf, scol, cnt[e][r], "a2")
         hold[(e, r)] = (dst, "land", a)
 
-    def pair(e, keep, go):
-        lo = min(keep, go)
-        dst = recv[keep][e]
-        a = room(dst, cnt[e][keep] + cnt[e][go])
-        put(0, cores[e], dst, "land", a, "zs", zoff[e][lo], cnt[e][keep] + cnt[e][go], "a1")
-        hold[(e, keep)] = (dst, "land", a + zoff[e][keep] - zoff[e][lo])
-        final(2, dst, e, go, "land", a + zoff[e][go] - zoff[e][lo])
-
+    inport = {}
     for e in range(n):
         c = cores[e]
         hold[(e, e)] = (c, "zs", zoff[e][e])
-        if e in ring:
-            i, m = ring.index(e), len(ring)
-            halves = [[ring[(i + j) % m] for j in range(1, 1 + m // 2)], [ring[(i + j) % m] for j in range(1 + m // 2, m)]]
-        else:
-            ks = [r for r in ring if by_cable_columns(e, r)]
-            halves = [ks[:(len(ks) + 1) // 2], ks[(len(ks) + 1) // 2:]]
-        for k, half in ((6, halves[0]), (2, halves[1])):
+        for k, half in ((6, halves[e][0]), (2, halves[e][1])):
             h = on(c, k)
             for a, b in _runs(sorted(half)):
                 put(0, c, h, "zs", zoff[e][a], "zs", zoff[e][a], zoff[e][b + 1] - zoff[e][a], "hand")
@@ -111,22 +141,36 @@ def make_plan(tables, cores, topo):
                     a = room(dst, cnt[e][r])
                     put(1, h, dst, "land", a, "zs", zoff[e][r], cnt[e][r], "a2")
                     hold[(e, r)] = (dst, "land", a)
-        if e in ring:
-            door = on(across(c), 0)
-            if door in chip_rank:
-                q = chip_rank[door]
-                pair(e, q, far[1] if q == far[0] else far[0])
-            else:
-                dst = door + (6 if (topo.chip(c) // 2) % 2 == 0 else 2)
-                w = cnt[e][far[0]] + cnt[e][far[1]]
-                a = room(dst, w)
-                put(0, c, dst, "land", a, "zs", zoff[e][far[0]], w, "a1")
-                for r in far:
-                    final(2, dst, e, r, "land", a + zoff[e][r] - zoff[e][far[0]])
-        else:
-            o = far[1] if e == far[0] else far[0]
-            final(0, c, e, chip_rank[on(across(c), 0)], "zs", zoff[e][chip_rank[on(across(c), 0)]])
-            pair(e, o, chip_rank[on(across(cores[o]), 0)])
+        if e in corner:
+            x, keep = at[across(c)], at[beside(c)]
+            go = at[across(cores[keep])]
+            final(0, c, e, x, "zs", zoff[e][x])
+            lo, w = min(keep, go), cnt[e][keep] + cnt[e][go]
+            dst = recv[keep][e]
+            a = room(dst, w)
+            put(0, c, dst, "land", a, "zs", zoff[e][lo], w, "a1")
+            hold[(e, keep)] = (dst, "land", a + zoff[e][keep] - zoff[e][lo])
+            final(2, dst, e, go, "land", a + zoff[e][go] - zoff[e][lo])
+            if keep in far:
+                inport[(keep, topo.die(c))] = inport.get((keep, topo.die(c)), 0) + w
+
+    lo = far[0]
+    for e in sorted([e for e in ring if e not in corner], key=lambda e: (-cnt[e][far[0]] - cnt[e][far[1]], e)):
+        door = across(cores[e])
+        cost = {}
+        for k in (6, 2):
+            d = topo.die(on(door, k))
+            cost[k] = max(inport.get((r, d), 0) + (0 if topo.mates(door, cores[r]) else cnt[e][r]) for r in far)
+        k = 6 if cost[6] <= cost[2] else 2
+        dst = on(door, k)
+        for r in far:
+            if not topo.mates(door, cores[r]):
+                inport[(r, topo.die(dst))] = inport.get((r, topo.die(dst)), 0) + cnt[e][r]
+        w = cnt[e][far[0]] + cnt[e][far[1]]
+        a = room(dst, w)
+        put(0, cores[e], dst, "land", a, "zs", zoff[e][lo], w, "a1")
+        for r in far:
+            final(2, dst, e, r, "land", a + zoff[e][r] - zoff[e][lo])
 
     jobs = {}
     for r in range(n):
@@ -177,7 +221,7 @@ def rank_program(g, core, T, topo):
         return p["expect"].get((core, sem), 0)
 
     def issue(stage):
-        for dst, dbuf, dcol, sbuf, scol, w, sem in mine.get(stage, []):
+        for dst, dbuf, dcol, sbuf, scol, w, sem in sorted(mine.get(stage, []), key=lambda x: x[0] // 8 == core // 8):
             rid, pid = topo.addr(dst, core)
             m = topo.mask(core, dst)
             g.remote_dma(out_ap=T[dbuf][:, dcol:dcol + w], in_ap=T[sbuf][:, scol:scol + w], remote_sem=T.sem[sem],

import comms_topo
from concourse.bass import DstId, RemoteDMATransfer

SCRATCH = {
    "zs": ("sbuf", [128, 279], "float32"),
    "land": ("sbuf", [128, 52], "float32"),
    "ybuf": ("sbuf", [128, 256], "float32"),
}
SEMAPHORES = ["ld", "hand", "a1", "a2", "col", "sent", "locg", "loc", "st"]

_PLAN = {}


def _bits(m):
    n = 0
    while m:
        n += m & 1
        m >>= 1
    return n


def _runs(rs):
    out = []
    for r in rs:
        if out and out[-1][1] + 1 == r:
            out[-1][1] = r
        else:
            out.append([r, r])
    return out


def _better(size, where, load):
    hi = max(load, key=lambda k: (load[k], -k))
    for a in sorted(e for e in where if where[e] == hi):
        for k in sorted(load):
            if k != hi:
                for b in [None] + sorted(e for e in where if where[e] == k):
                    d = size[a] - (size[b] if b is not None else 0)
                    if d > 0 and load[k] + d < load[hi]:
                        return a, b, hi, k, d
    return None


def _share(size, load):
    where = {}
    for e in sorted(size, key=lambda e: (-size[e], e)):
        k = min(load, key=lambda k: (load[k], k))
        load[k] += size[e]
        where[e] = k
    mv = _better(size, where, load)
    while mv:
        a, b, hi, k, d = mv
        where[a] = k
        if b is not None:
            where[b] = hi
        load[hi] -= d
        load[k] += d
        mv = _better(size, where, load)
    return where


def make_plan(tables, cores, topo):
    route = tables["ROUTE"]
    n, nt = len(cores), len(route[0])
    cnt = [[0] * n for _ in range(n)]
    wide = [[0] * n for _ in range(n)]
    for r in range(n):
        for t in range(nt):
            cnt[route[r][t][0]][r] += 1
            if t == 0 or route[r][t - 1][0] != route[r][t][0]:
                wide[route[r][t][0]][r] += 1
    zoff = [[sum(cnt[e][:r]) for r in range(n + 1)] for e in range(n)]

    def on(c, k):
        return c - c % 8 + k

    def across(c):
        return (3 - topo.host(c)) * 128 + c % 128

    def beside(c):
        return (topo.host(c) ^ 1) * 128 + c % 128

    ring = [i for i in range(n) if topo.rack(topo.host(cores[i])) == 1]
    far = [i for i in range(n) if i not in ring]
    at = {cores[i]: i for i in range(n)}
    corner = [i for i in range(n) if across(cores[i]) in at]

    blocks = {}
    expect = {}
    top = {}
    hold = {}

    def put(stage, src, dst, dbuf, dcol, sbuf, scol, w, sem):
        blocks.setdefault(src, {}).setdefault(stage, []).append((dst, dbuf, dcol, sbuf, scol, w, sem))
        expect[(dst, sem)] = expect.get((dst, sem), 0) + _bits(topo.mask(src, dst))

    def room(c, w):
        a = top.get(c, 0)
        top[c] = a + w
        return a

    halves = []
    for e in range(n):
        if e in ring:
            i, m = ring.index(e), len(ring)
            rs = [ring[(i + j) % m] for j in range(1, m)]
            if e in corner:
                rs.remove(at[beside(cores[e])])
        else:
            rs = [r for r in ring if r not in corner]
        halves.append([rs[:(len(rs) + 1) // 2], rs[(len(rs) + 1) // 2:]])

    recv = []
    for r in range(n):
        load = {k: 0 for k in range(8)}
        load[4] = wide[r][r] + 2 + sum(len(_runs(sorted(h))) for h in halves[r]) + (2 if r in corner else 1)
        load[6], load[2] = len(halves[r][0]), len(halves[r][1])
        size = {e: wide[e][r] + (1 if e in corner and at[beside(cores[e])] == r else 0)
                for e in range(n) if e != r and not (e in far and r not in corner)}
        recv.append({e: on(cores[r], k) for e, k in _share(size, load).items()})

    def final(stage, src, e, r, sbuf, scol):
        dst = recv[r][e]
        a = room(dst, cnt[e][r])
        put(stage, src, dst, "land", a, sbuf, scol, cnt[e][r], "a2")
        hold[(e, r)] = (dst, "land", a)

    inport = {}
    for e in range(n):
        c = cores[e]
        hold[(e, e)] = (c, "zs", zoff[e][e])
        for k, half in ((6, halves[e][0]), (2, halves[e][1])):
            h = on(c, k)
            for a, b in _runs(sorted(half)):
                put(0, c, h, "zs", zoff[e][a], "zs", zoff[e][a], zoff[e][b + 1] - zoff[e][a], "hand")
            for r in half:
                if e in ring:
                    final(1, h, e, r, "zs", zoff[e][r])
                else:
                    dst = on(across(cores[r]), 0 if e == far[0] else 4)
                    a = room(dst, cnt[e][r])
                    put(1, h, dst, "land", a, "zs", zoff[e][r], cnt[e][r], "a2")
                    hold[(e, r)] = (dst, "land", a)
        if e in corner:
            x, keep = at[across(c)], at[beside(c)]
            go = at[across(cores[keep])]
            final(0, c, e, x, "zs", zoff[e][x])
            lo, w = min(keep, go), cnt[e][keep] + cnt[e][go]
            dst = recv[keep][e]
            a = room(dst, w)
            put(0, c, dst, "land", a, "zs", zoff[e][lo], w, "a1")
            hold[(e, keep)] = (dst, "land", a + zoff[e][keep] - zoff[e][lo])
            final(2, dst, e, go, "land", a + zoff[e][go] - zoff[e][lo])
            if keep in far:
                inport[(keep, topo.die(c))] = inport.get((keep, topo.die(c)), 0) + w

    lo = far[0]
    for e in sorted([e for e in ring if e not in corner], key=lambda e: (-cnt[e][far[0]] - cnt[e][far[1]], e)):
        door = across(cores[e])
        cost = {}
        for k in (6, 2):
            d = topo.die(on(door, k))
            cost[k] = max(inport.get((r, d), 0) + (0 if topo.mates(door, cores[r]) else cnt[e][r]) for r in far)
        k = 6 if cost[6] <= cost[2] else 2
        dst = on(door, k)
        for r in far:
            if not topo.mates(door, cores[r]):
                inport[(r, topo.die(dst))] = inport.get((r, topo.die(dst)), 0) + cnt[e][r]
        w = cnt[e][far[0]] + cnt[e][far[1]]
        a = room(dst, w)
        put(0, cores[e], dst, "land", a, "zs", zoff[e][lo], w, "a1")
        for r in far:
            final(2, dst, e, r, "land", a + zoff[e][r] - zoff[e][lo])

    jobs = {}
    for r in range(n):
        seen = [0] * n
        for t in range(nt):
            e = route[r][t][0]
            c, buf, col = hold[(e, r)]
            col += seen[e]
            seen[e] += 1
            lst = jobs.setdefault((c, r), [])
            if lst and t and route[r][t - 1][0] == e:
                lst[-1] = (lst[-1][0], lst[-1][1] + 1, buf, lst[-1][3])
            else:
                lst.append((t, 1, buf, col))
    cols, copies = {}, {}
    for (c, r), lst in sorted(jobs.items()):
        if c == cores[r]:
            copies[r] = lst
            continue
        cap = _bits(topo.mask(c, cores[r]))
        calls = cols.setdefault(c, (cores[r], []))[1]
        for w in sorted(set(x[1] for x in lst)):
            same = [x for x in lst if x[1] == w]
            i = 0
            while i < len(same):
                m = min(cap, len(same) - i)
                per = 1
                while per * 2 * m <= cap:
                    per *= 2
                calls.append([(((1 << per) - 1) << (j * per),) + same[i + j] for j in range(m)])
                expect[(cores[r], "col")] = expect.get((cores[r], "col"), 0) + per * m
                i += m
    return {"blocks": blocks, "expect": expect, "cols": cols, "copies": copies, "top": top,
            "used": [zoff[e][n] for e in range(n)]}


def rank_program(g, core, T, topo):
    if "p" not in _PLAN:
        _PLAN["p"] = make_plan(T.tables, list(T.cores), topo)
    p = _PLAN["p"]
    rank = T.rank_of(core)
    mine = p["blocks"].get(core, {})
    if rank is None and not mine and core not in p["cols"]:
        return
    sent = [0]

    def need(sem):
        return p["expect"].get((core, sem), 0)

    def issue(stage):
        for dst, dbuf, dcol, sbuf, scol, w, sem in sorted(mine.get(stage, []), key=lambda x: x[0] // 8 == core // 8):
            rid, pid = topo.addr(dst, core)
            m = topo.mask(core, dst)
            g.remote_dma(out_ap=T[dbuf][:, dcol:dcol + w], in_ap=T[sbuf][:, scol:scol + w], remote_sem=T.sem[sem],
                         local_sem=T.sem.sent, pid=pid, routing_id=rid, dma_engine_mask=m)
            sent[0] += _bits(m)

    if rank is not None:
        w = p["used"][rank]
        g.sync.dma_start(T.zs[:, 0:w], T.z[:, 0:w]).then_inc(T.sem.ld, 16)
        g.wait_ge(T.sem.ld, 16)
        issue(0)
    if need("hand"):
        g.wait_ge(T.sem.hand, need("hand"))
        issue(1)
    if need("a1"):
        g.wait_ge(T.sem.a1, need("a1"))
        issue(2)
    if need("a2"):
        g.wait_ge(T.sem.a2, need("a2"))
    if core in p["cols"]:
        dst, calls = p["cols"][core]
        rid, pid = topo.addr(dst, core)
        for call in calls:
            g.remote_dma_fused([RemoteDMATransfer(dst_ids=[DstId(rid=rid, pnc=pid)], dma_engine_mask=m, remote_sem=T.sem.col,
                                                  src=T[buf][:, col:col + w], dst=T.ybuf[:, t:t + w])
                                for m, t, w, buf, col in call], local_sem=T.sem.sent)
            sent[0] += sum(_bits(x[0]) for x in call)
    if rank is not None:
        for q in (g.sync, g.scalar):
            q.wait_ge(T.sem.ld, 16)
            for s in ("a1", "a2"):
                if need(s):
                    q.wait_ge(T.sem[s], need(s))
        qs = [(g.sync, T.sem.loc), (g.scalar, T.sem.loc), (g, T.sem.locg)]
        done = [0, 0, 0]
        for k, (t, w, buf, col) in enumerate(p["copies"][rank]):
            q, s = qs[k % 3]
            q.dma_start(T.ybuf[:, t:t + w], T[buf][:, col:col + w]).then_inc(s, 16)
            done[k % 3] += 16
        g.wait_ge(T.sem.locg, done[2])
        g.wait_ge(T.sem.loc, done[0] + done[1])
        g.wait_ge(T.sem.col, need("col"))
        g.dma_start(T.y[:, :], T.ybuf[:, :]).then_inc(T.sem.st, 16)
        g.wait_ge(T.sem.st, 16)
    g.wait_ge(T.sem.sent, sent[0])
